import numpy as np
import ml_dtypes


def mxq(x, axis, fmt="e4m3"):
    dtype, down = {"e4m3": (ml_dtypes.float8_e4m3fn, 7), "e5m2": (ml_dtypes.float8_e5m2, 14)}[fmt]
    v = np.moveaxis(np.asarray(x, np.float32).astype(ml_dtypes.bfloat16).astype(np.float64), axis, -1)
    blocks = v.reshape(v.shape[:-1] + (-1, 32))
    amax = np.abs(blocks).max(-1, keepdims=True)
    byte = np.maximum(np.where(amax > 0, np.frexp(amax)[1] - 1 + 127, 0) - down, 1)
    scale = np.exp2(byte - 127.0)
    codes = (blocks / scale).astype(np.float32).astype(dtype).astype(np.float64)
    return np.moveaxis((codes * scale).reshape(v.shape), -1, axis)


WIDE = False


def mx_kscale(k):
    if not WIDE:
        return np.ones(k)
    levels = np.array([10, -10, 5, -5, 0])
    if k % 512:
        return np.exp2(np.random.permutation(np.resize(levels, k // 32))).repeat(32)
    a = np.empty((k // 512, 16))
    for p in range(k // 512):
        a[p, :8] = np.random.permutation(np.resize(levels, 8))
        for g in range(8):
            far = levels[np.abs(levels - a[p, g]) >= 10]
            a[p, g + 8] = far[np.random.randint(len(far))]
    return np.exp2(a.ravel()).repeat(32)


def f64(x):
    return np.asarray(x).astype(np.float64)


def striped(idx):
    return np.tile(idx.reshape(-1, 16).T, (8, 1)).astype(np.uint16)


def unstriped(offs):
    return offs[:16].T.reshape(-1).astype(np.int64)


def relu(v):
    return np.maximum(v, 0.0)


K, T, S, V, H, N = 1024, 1024, 512, 256, 512, 256


def setup_inputs():
    n = np.random.standard_normal
    s = mx_kscale(K)[:, None]
    u = mx_kscale(H)
    return {
        "xT": (n((K, T)) * s).astype(np.float32),
        "w1": (n((K, H)) / np.sqrt(K) / s * u).astype(np.float32),
        "w2": (n((H, N)) / np.sqrt(2 * H) / u[:, None]).astype(np.float32),
        "w3": (n((H, N)) / np.sqrt(2 * H) / u[:, None]).astype(np.float32),
        "offs": striped(np.random.permutation(T)[:S]),
        "cen": striped(np.random.permutation(S)[:V]),
        "pos1": striped(np.random.permutation(S)[:V]),
        "pos2": striped(np.random.permutation(S)[:V]),
    }


def reference(xT, w1, w2, w3, offs, cen, pos1, pos2):
    xq = mxq(f64(xT)[:, unstriped(offs)], 0, "e4m3")
    h = relu(mxq(f64(w1), 0, "e4m3").T @ xq)
    hc = h[:, unstriped(cen)]
    z = np.maximum(h[:, unstriped(pos1)], h[:, unstriped(pos2)])
    return mxq(f64(w2), 0, "e4m3").T @ mxq(hc, 0, "e4m3") + mxq(f64(w3), 0, "e4m3").T @ mxq(z, 0, "e4m3")

@@ -1,0 +1,227 @@
+from contextlib import ExitStack
+
+import concourse.mybir as mybir
+
+K, T, S, V, H, N = 1024, 1024, 512, 256, 512, 256
+FLOPS = 2 * K * H * S + 2 * 2 * H * N * V
+
+F32 = mybir.dt.float32
+BF16 = mybir.dt.bfloat16
+U32 = mybir.dt.uint32
+I32 = mybir.dt.int32
+U16 = mybir.dt.uint16
+U8 = mybir.dt.uint8
+FP8X4 = mybir.dt.float8_e4m3fn_x4
+COPY = mybir.ActivationFunctionType.Copy
+RELU = mybir.ActivationFunctionType.Relu
+MAX = mybir.AluOpType.max
+
+P = 128
+PACK = 4
+K_PASS = P * PACK
+PASSES = K // K_PASS
+X_CHUNKS = ((256, 256, 256, 256), (256, 256, 256, 256))
+X_SHARES = ((96, 96, 96, 160), (0, 96, 96, 160))
+W_CHUNK = 256
+V_HALF = V // 2
+
+
+def cast(nc, engine, out, in_):
+    if engine == "vector":
+        nc.vector.tensor_copy(out=out, in_=in_)
+    else:
+        nc.scalar.activation(out, in_, COPY)
+
+
+def interleave(nc, engine, grouped, planes, lo, hi, run):
+    cast(
+        nc,
+        engine,
+        grouped[:, lo:hi, :].rearrange("p (c i) j -> p c j i", i=run),
+        planes[:, :, lo:hi].rearrange("p j (c i) -> p c j i", i=run),
+    )
+
+
+def quantize(nc, codes, scales, grouped):
+    nc.vector.quantize_mx(out=codes.bitcast(FP8X4), scales=scales, in_=grouped)
+
+
+def mx_pass(nc, out, lhs_codes, lhs_scales, rhs_codes, rhs_scales, start, stop):
+    nc.tensor.matmul_mx(
+        out=out,
+        lhsT=lhs_codes.bitcast(FP8X4),
+        lhsT_scale=lhs_scales,
+        rhs=rhs_codes.bitcast(FP8X4),
+        rhs_scale=rhs_scales,
+        start=start,
+        stop=stop,
+    )
+
+
+def tile_picked_sagecat_max_e_kernel(tc, xT, w1, w2, w3, offs, cen, pos1, pos2, out):
+    nc = tc.nc
+    with ExitStack() as ctx:
+        lists = ctx.enter_context(tc.tile_pool(name="lists", bufs=1))
+        pool = ctx.enter_context(tc.tile_pool(name="sbuf", bufs=1))
+        psum = ctx.enter_context(tc.psum_pool(name="psum", bufs=1))
+
+        def sb(shape, dtype, name, tag=None):
+            return pool.tile(shape, dtype, name=name, tag=tag or name, align_bytes=64)
+
+        def load_list(src, name):
+            tile = lists.tile(list(src.shape), U16, name=name, tag=name)
+            nc.sync.dma_start(tile[:], src)
+            return tile
+
+        x_raw = {}
+        for g in range(PASSES):
+            rows = xT[g * K_PASS : (g + 1) * K_PASS, :].rearrange("(p j) c -> p j c", j=PACK)
+            for c, width in enumerate(X_CHUNKS[g]):
+                lo = sum(X_CHUNKS[g][:c])
+                x_raw[g, c] = sb([P, PACK, width], F32, f"x_raw{g}{c}")
+                nc.sync.dma_start(out=x_raw[g, c][:], in_=rows[:, :, lo : lo + width])
+            if g == 0:
+                offs_sb = load_list(offs, "offs_sb")
+        w1_raw = {}
+        for g in range(PASSES):
+            rows = w1[g * K_PASS : (g + 1) * K_PASS, :].rearrange("(p j) c -> p j c", j=PACK)
+            for c in range(H // W_CHUNK):
+                w1_raw[g, c] = sb([P, PACK, W_CHUNK], F32, f"w1_raw{g}{c}")
+                nc.sync.dma_start(out=w1_raw[g, c][:], in_=rows[:, :, c * W_CHUNK : (c + 1) * W_CHUNK])
+        pos1_sb = load_list(pos1, "pos1_sb")
+        pos2_sb = load_list(pos2, "pos2_sb")
+        cen_sb = load_list(cen, "cen_sb")
+        w3_raw = sb([P, PACK, N], F32, "w3_raw")
+        nc.sync.dma_start(out=w3_raw[:], in_=w3.rearrange("(p j) c -> p j c", j=PACK))
+        w2_raw = sb([P, PACK, N], F32, "w2_raw")
+        nc.sync.dma_start(out=w2_raw[:], in_=w2.rearrange("(p j) c -> p j c", j=PACK))
+
+        x_scales = sb([P, T], U8, "x_scales")
+        nc.vector.memset(x_scales[:].bitcast(I32), 0)
+        picked_codes = []
+        for g in range(PASSES):
+            x_codes = sb([P, T], U32, f"x_codes{g}")
+            for c, width in enumerate(X_CHUNKS[g]):
+                lo = sum(X_CHUNKS[g][:c])
+                cols = slice(lo, lo + width)
+                share = X_SHARES[g][c]
+                grouped = sb([P, width, PACK], BF16, f"x_grouped{g}{c}")
+                if share:
+                    interleave(nc, "vector", grouped, x_raw[g, c], 0, share, 4)
+                interleave(nc, "scalar", grouped, x_raw[g, c], share, width, 4)
+                quantize(nc, x_codes[:, cols], x_scales[4 * g :, cols], grouped[:].rearrange("p c j -> p (c j)"))
+            picked = sb([P, S], U32, f"picked_codes{g}")
+            nc.vector.tensor_copy(out=picked[:], in_=x_codes[:].indirect(offs_sb[:]))
+            picked_codes.append(picked)
+        picked_scales = sb([P, S], U8, "picked_scales")
+        nc.vector.tensor_copy(out=picked_scales[:], in_=x_scales[:].indirect(offs_sb[:]))
+
+        m_chunk = W_CHUNK // PACK
+        w1_grouped = {}
+        for g in range(PASSES):
+            for u in range(2):
+                w1_grouped[g, u] = sb([P, 2, P, PACK], BF16, f"w1_grouped{g}{u}")
+            for c in range(H // W_CHUNK):
+                src = w1_raw[g, c][:].rearrange("p j (m t) -> p m j t", t=PACK)
+                for u in range(2):
+                    last = g == PASSES - 1 and c == H // W_CHUNK - 1
+                    cast(
+                        nc,
+                        "vector" if last and u == 0 else "scalar",
+                        w1_grouped[g, u][:, :, c * m_chunk : (c + 1) * m_chunk, :].rearrange("p t m j -> p m j t"),
+                        src[:, :, :, 2 * u : 2 * u + 2],
+                    )
+        w1_codes, w1_scales = {}, {}
+        for u in range(2):
+            for g in range(PASSES):
+                tag = "w1_grouped10" if (g, u) == (0, 1) else None
+                codes = sb([P, 2, P], U32, f"w1_codes{g}{u}", tag)
+                scales = sb([P, 2, P], U8, f"w1_scales{g}{u}")
+                grouped = w1_grouped[g, u]
+                if g == PASSES - 1 and u == 0:
+                    for e in range(2):
+                        quantize(nc, codes[:, e, :], scales[:, e, :], grouped[:, e, :, :].rearrange("p m j -> p (m j)"))
+                else:
+                    quantize(
+                        nc,
+                        codes[:].rearrange("p t m -> p (t m)"),
+                        scales[:].rearrange("p t m -> p (t m)"),
+                        grouped[:].rearrange("p t m j -> p (t m j)"),
+                    )
+                for e in range(2):
+                    w1_codes[g, 2 * u + e] = codes[:, e, :]
+                    w1_scales[g, 2 * u + e] = scales[:, e, :]
+
+        h = []
+        for t in range(PACK):
+            h_t = sb([P, S], F32, f"h{t}")
+            pieces = [slice(0, S // 2), slice(S // 2, S)] if t == 0 else [slice(0, S)]
+            banks = [psum.tile([P, cols.stop - cols.start], F32, name=f"h_bank{t}{n}", tag=f"h_bank{t}{n}") for n, cols in enumerate(pieces)]
+            for g in range(PASSES):
+                for bank, cols in zip(banks, pieces):
+                    mx_pass(nc, bank[:], w1_codes[g, t], w1_scales[g, t], picked_codes[g][:, cols], picked_scales[4 * g :, cols], g == 0, g == PASSES - 1)
+            for n, (bank, cols) in enumerate(zip(banks, pieces)):
+                if n == 1:
+                    nc.vector.tensor_scalar_max(h_t[:, cols], bank[:], 0.0)
+                else:
+                    nc.scalar.activation(h_t[:, cols], bank[:], RELU)
+            h.append(h_t)
+
+        first = sb([P, PACK, V], BF16, "first")
+        second = sb([P, PACK, V], BF16, "second")
+        for t in range(PACK):
+            nc.vector.tensor_copy(out=first[:, t, :], in_=h[t][:].indirect(pos1_sb[:]))
+            nc.vector.tensor_copy(out=second[:, t, :], in_=h[t][:].indirect(pos2_sb[:]))
+
+        out_w = []
+        for raw, name, tag in ((w3_raw, "w3", "picked_codes1"), (w2_raw, "w2", "w1_codes11")):
+            grouped = sb([P, N, PACK], BF16, name + "_grouped", tag)
+            interleave(nc, "scalar", grouped, raw, 0, N, 4)
+            codes = sb([P, N], U32, name + "_codes")
+            scales = sb([P, N], U8, name + "_scales")
+            quantize(nc, codes[:], scales[:], grouped[:].rearrange("p c j -> p (c j)"))
+            out_w.append((codes, scales))
+        (w3_codes, w3_scales), (w2_codes, w2_scales) = out_w
+
+        z = sb([P, PACK, V], BF16, "z")
+        nc.vector.tensor_tensor(z[:], first[:], second[:], MAX)
+        z_grouped = sb([P, V, PACK], BF16, "z_grouped")
+        interleave(nc, "scalar", z_grouped, z, 0, V, 8)
+        z_codes = sb([P, V], U32, "z_codes")
+        z_scales = sb([P, V], U8, "z_scales")
+
+        out_rows = out.rearrange("(a p) v -> p a v", p=P)
+        for half in range(2):
+            cols = slice(half * V_HALF, (half + 1) * V_HALF)
+            offsets = cen_sb[:, half * (V_HALF // 16) : (half + 1) * (V_HALF // 16)]
+            own = sb([P, PACK, V_HALF], BF16, f"own{half}", "first" if half == 0 else "z_grouped")
+            for t in range(PACK):
+                nc.vector.tensor_copy(out=own[:, t, :], in_=h[t][:].indirect(offsets))
+            if half == 0:
+                quantize(nc, z_codes[:], z_scales[:], z_grouped[:].rearrange("p c j -> p (c j)"))
+            own_grouped = sb([P, V_HALF, PACK], BF16, f"own_grouped{half}")
+            interleave(nc, "scalar" if half == 0 else "vector", own_grouped, own, 0, V_HALF, 8)
+            own_codes = sb([P, V_HALF], U32, f"own_codes{half}")
+            own_scales = sb([P, V_HALF], U8, f"own_scales{half}")
+            quantize(nc, own_codes[:], own_scales[:], own_grouped[:].rearrange("p c j -> p (c j)"))
+
+            if half == 0:
+                shared = psum.tile([P, 2, V_HALF], F32, name="out_bank0", tag="out_bank0")
+                banks = [shared[:, a, :] for a in range(2)]
+            else:
+                banks = [psum.tile([P, V_HALF], F32, name=f"out_bank1{a}", tag=f"out_bank1{a}")[:] for a in range(2)]
+            for a in range(2):
+                rows = slice(a * P, (a + 1) * P)
+                mx_pass(nc, banks[a], w3_codes[:, rows], w3_scales[:, rows], z_codes[:, cols], z_scales[:, cols], True, False)
+                mx_pass(nc, banks[a], w2_codes[:, rows], w2_scales[:, rows], own_codes[:], own_scales[:], False, True)
+            if half == 0:
+                result = sb([P, 2, V_HALF], F32, "result0")
+                nc.scalar.copy(result[:], shared[:])
+                nc.sync.dma_start(out=out_rows[:, :, cols], in_=result[:])
+            else:
+                result_a = sb([P, V_HALF], F32, "result10")
+                nc.vector.tensor_copy(out=result_a[:], in_=banks[0])
+                nc.sync.dma_start(out=out_rows[:, 0, cols], in_=result_a[:])
+                result_b = sb([P, V_HALF], F32, "result11")
+                nc.scalar.copy(result_b[:], banks[1])
+                nc.scalar.dma_start(out=out_rows[:, 1, cols], in_=result_b[:])

@@ -117,40 +117,31 @@ def tile_picked_sagecat_max_e_kernel(tc, xT, w1, w2, w3, offs, cen, pos1, pos2, 
         nc.vector.tensor_copy(out=picked_scales[:], in_=x_scales[:].indirect(offs_sb[:]))
 
         m_chunk = W_CHUNK // PACK
-        w1_grouped = {}
+        w1_grouped = []
         for g in range(PASSES):
-            for u in range(2):
-                w1_grouped[g, u] = sb([P, 2, P, PACK], BF16, f"w1_grouped{g}{u}")
+            grouped = sb([P, PACK, P, PACK], BF16, f"w1_grouped{g}")
             for c in range(H // W_CHUNK):
                 src = w1_raw[g, c][:].rearrange("p j (m t) -> p m j t", t=PACK)
-                for u in range(2):
-                    last = g == PASSES - 1 and c == H // W_CHUNK - 1
-                    cast(
-                        nc,
-                        "vector" if last and u == 0 else "scalar",
-                        w1_grouped[g, u][:, :, c * m_chunk : (c + 1) * m_chunk, :].rearrange("p t m j -> p m j t"),
-                        src[:, :, :, 2 * u : 2 * u + 2],
-                    )
-        w1_codes, w1_scales = {}, {}
-        for u in range(2):
-            for g in range(PASSES):
-                tag = "w1_grouped10" if (g, u) == (0, 1) else None
-                codes = sb([P, 2, P], U32, f"w1_codes{g}{u}", tag)
-                scales = sb([P, 2, P], U8, f"w1_scales{g}{u}")
-                grouped = w1_grouped[g, u]
-                if g == PASSES - 1 and u == 0:
-                    for e in range(2):
-                        quantize(nc, codes[:, e, :], scales[:, e, :], grouped[:, e, :, :].rearrange("p m j -> p (m j)"))
+                dst = grouped[:, :, c * m_chunk : (c + 1) * m_chunk, :].rearrange("p t m j -> p m j t")
+                if g == PASSES - 1:
+                    cast(nc, "vector" if c == H // W_CHUNK - 1 else "scalar", dst[:, :, :, 0:2], src[:, :, :, 0:2])
+                    cast(nc, "scalar", dst[:, :, :, 2:4], src[:, :, :, 2:4])
                 else:
-                    quantize(
-                        nc,
-                        codes[:].rearrange("p t m -> p (t m)"),
-                        scales[:].rearrange("p t m -> p (t m)"),
-                        grouped[:].rearrange("p t m j -> p (t m j)"),
-                    )
-                for e in range(2):
-                    w1_codes[g, 2 * u + e] = codes[:, e, :]
-                    w1_scales[g, 2 * u + e] = scales[:, e, :]
+                    cast(nc, "scalar", dst, src)
+            w1_grouped.append(grouped)
+        w1_codes, w1_scales = {}, {}
+        for g, t0, t1, tag in ((0, 0, 2, None), (1, 0, 1, None), (1, 1, 2, None), (1, 2, 4, None), (0, 2, 4, "w1_grouped1")):
+            codes = sb([P, t1 - t0, P], U32, f"w1_codes{g}{t0}", tag)
+            scales = sb([P, t1 - t0, P], U8, f"w1_scales{g}{t0}")
+            quantize(
+                nc,
+                codes[:].rearrange("p t m -> p (t m)"),
+                scales[:].rearrange("p t m -> p (t m)"),
+                w1_grouped[g][:, t0:t1, :, :].rearrange("p t m j -> p (t m j)"),
+            )
+            for t in range(t0, t1):
+                w1_codes[g, t] = codes[:, t - t0, :]
+                w1_scales[g, t] = scales[:, t - t0, :]
 
         h = []
         for t in range(PACK):
@@ -174,7 +165,7 @@ def tile_picked_sagecat_max_e_kernel(tc, xT, w1, w2, w3, offs, cen, pos1, pos2, 
             nc.vector.tensor_copy(out=second[:, t, :], in_=h[t][:].indirect(pos2_sb[:]))
 
         out_w = []
-        for raw, name, tag in ((w3_raw, "w3", "picked_codes1"), (w2_raw, "w2", "w1_codes11")):
+        for raw, name, tag in ((w3_raw, "w3", "picked_codes1"), (w2_raw, "w2", "w1_codes12")):
             grouped = sb([P, N, PACK], BF16, name + "_grouped", tag)
             interleave(nc, "scalar", grouped, raw, 0, N, 4)
             codes = sb([P, N], U32, name + "_codes")
@@ -184,9 +175,11 @@ def tile_picked_sagecat_max_e_kernel(tc, xT, w1, w2, w3, offs, cen, pos1, pos2, 
         (w3_codes, w3_scales), (w2_codes, w2_scales) = out_w
 
         z = sb([P, PACK, V], BF16, "z")
-        nc.vector.tensor_tensor(z[:], first[:], second[:], MAX)
         z_grouped = sb([P, V, PACK], BF16, "z_grouped")
-        interleave(nc, "scalar", z_grouped, z, 0, V, 8)
+        for lo in range(0, V, V_HALF):
+            hi = lo + V_HALF
+            nc.vector.tensor_tensor(z[:, :, lo:hi], first[:, :, lo:hi], second[:, :, lo:hi], MAX)
+            interleave(nc, "scalar", z_grouped, z, lo, hi, 4)
         z_codes = sb([P, V], U32, "z_codes")
         z_scales = sb([P, V], U8, "z_scales")
 
@@ -200,28 +193,31 @@ def tile_picked_sagecat_max_e_kernel(tc, xT, w1, w2, w3, offs, cen, pos1, pos2, 
             if half == 0:
                 quantize(nc, z_codes[:], z_scales[:], z_grouped[:].rearrange("p c j -> p (c j)"))
             own_grouped = sb([P, V_HALF, PACK], BF16, f"own_grouped{half}")
-            interleave(nc, "scalar" if half == 0 else "vector", own_grouped, own, 0, V_HALF, 8)
+            pieces = [(0, V_HALF)] if half == 0 else [(0, V_HALF // 2), (V_HALF // 2, V_HALF)]
+            for lo, hi in pieces:
+                interleave(nc, "scalar" if half == 0 else "vector", own_grouped, own, lo, hi, 4)
             own_codes = sb([P, V_HALF], U32, f"own_codes{half}")
             own_scales = sb([P, V_HALF], U8, f"own_scales{half}")
-            quantize(nc, own_codes[:], own_scales[:], own_grouped[:].rearrange("p c j -> p (c j)"))
+            for lo, hi in pieces:
+                quantize(nc, own_codes[:, lo:hi], own_scales[:, lo:hi], own_grouped[:, lo:hi, :].rearrange("p c j -> p (c j)"))
 
-            if half == 0:
-                shared = psum.tile([P, 2, V_HALF], F32, name="out_bank0", tag="out_bank0")
-                banks = [shared[:, a, :] for a in range(2)]
-            else:
-                banks = [psum.tile([P, V_HALF], F32, name=f"out_bank1{a}", tag=f"out_bank1{a}")[:] for a in range(2)]
+            bank_tags = ("h_bank00", "h_bank01") if half == 0 else ("out_bank0", "out_bank1")
+            banks = [psum.tile([P, V_HALF], F32, name=f"out_bank{half}{a}", tag=bank_tags[a]) for a in range(2)]
             for a in range(2):
                 rows = slice(a * P, (a + 1) * P)
-                mx_pass(nc, banks[a], w3_codes[:, rows], w3_scales[:, rows], z_codes[:, cols], z_scales[:, cols], True, False)
-                mx_pass(nc, banks[a], w2_codes[:, rows], w2_scales[:, rows], own_codes[:], own_scales[:], False, True)
+                mx_pass(nc, banks[a][:], w3_codes[:, rows], w3_scales[:, rows], z_codes[:, cols], z_scales[:, cols], True, False)
+            for a in range(2):
+                rows = slice(a * P, (a + 1) * P)
+                mx_pass(nc, banks[a][:], w2_codes[:, rows], w2_scales[:, rows], own_codes[:], own_scales[:], False, True)
             if half == 0:
                 result = sb([P, 2, V_HALF], F32, "result0")
-                nc.scalar.copy(result[:], shared[:])
+                for a in range(2):
+                    nc.scalar.copy(result[:, a, :], banks[a][:])
                 nc.sync.dma_start(out=out_rows[:, :, cols], in_=result[:])
             else:
                 result_a = sb([P, V_HALF], F32, "result10")
-                nc.vector.tensor_copy(out=result_a[:], in_=banks[0])
+                nc.vector.tensor_copy(out=result_a[:], in_=banks[0][:])
                 nc.sync.dma_start(out=out_rows[:, 0, cols], in_=result_a[:])
                 result_b = sb([P, V_HALF], F32, "result11")
-                nc.scalar.copy(result_b[:], banks[1])
+                nc.scalar.copy(result_b[:], banks[1][:])
                 nc.scalar.dma_start(out=out_rows[:, 1, cols], in_=result_b[:])

@@ -20,9 +20,9 @@ P = 128
 PACK = 4
 K_PASS = P * PACK
 PASSES = K // K_PASS
-X_CHUNKS = ((256, 256, 256, 256), (256, 256, 256, 256))
-X_SHARES = ((96, 96, 96, 160), (0, 96, 96, 160))
-W_CHUNK = 256
+X_SHARES = (640, 640, 640, 512)
+W_FIRST_SHARE = 80
+W_SECOND_SHARE = 64
 V_HALF = V // 2
 
 
@@ -73,21 +73,20 @@ def tile_picked_sagecat_max_e_kernel(tc, xT, w1, w2, w3, offs, cen, pos1, pos2, 
             nc.sync.dma_start(tile[:], src)
             return tile
 
-        x_raw = {}
+        x_raw = []
         for g in range(PASSES):
             rows = xT[g * K_PASS : (g + 1) * K_PASS, :].rearrange("(p j) c -> p j c", j=PACK)
-            for c, width in enumerate(X_CHUNKS[g]):
-                lo = sum(X_CHUNKS[g][:c])
-                x_raw[g, c] = sb([P, PACK, width], F32, f"x_raw{g}{c}")
-                nc.sync.dma_start(out=x_raw[g, c][:], in_=rows[:, :, lo : lo + width])
-            if g == 0:
-                offs_sb = load_list(offs, "offs_sb")
-        w1_raw = {}
+            for u in range(2):
+                raw = sb([P, 2, T], F32, f"x_raw{g}{u}")
+                nc.sync.dma_start(out=raw[:], in_=rows[:, 2 * u : 2 * u + 2, :])
+                x_raw.append(raw)
+                if (g, u) == (0, 0):
+                    offs_sb = load_list(offs, "offs_sb")
+        w1_raw = []
         for g in range(PASSES):
-            rows = w1[g * K_PASS : (g + 1) * K_PASS, :].rearrange("(p j) c -> p j c", j=PACK)
-            for c in range(H // W_CHUNK):
-                w1_raw[g, c] = sb([P, PACK, W_CHUNK], F32, f"w1_raw{g}{c}")
-                nc.sync.dma_start(out=w1_raw[g, c][:], in_=rows[:, :, c * W_CHUNK : (c + 1) * W_CHUNK])
+            raw = sb([P, PACK, H], F32, f"w1_raw{g}")
+            nc.sync.dma_start(out=raw[:], in_=w1[g * K_PASS : (g + 1) * K_PASS, :].rearrange("(p j) c -> p j c", j=PACK))
+            w1_raw.append(raw)
         pos1_sb = load_list(pos1, "pos1_sb")
         pos2_sb = load_list(pos2, "pos2_sb")
         cen_sb = load_list(cen, "cen_sb")
@@ -96,52 +95,73 @@ def tile_picked_sagecat_max_e_kernel(tc, xT, w1, w2, w3, offs, cen, pos1, pos2, 
         w2_raw = sb([P, PACK, N], F32, "w2_raw")
         nc.sync.dma_start(out=w2_raw[:], in_=w2.rearrange("(p j) c -> p j c", j=PACK))
 
-        x_scales = sb([P, T], U8, "x_scales")
-        nc.vector.memset(x_scales[:].bitcast(I32), 0)
-        picked_codes = []
-        for g in range(PASSES):
-            x_codes = sb([P, T], U32, f"x_codes{g}")
-            for c, width in enumerate(X_CHUNKS[g]):
-                lo = sum(X_CHUNKS[g][:c])
-                cols = slice(lo, lo + width)
-                share = X_SHARES[g][c]
-                grouped = sb([P, width, PACK], BF16, f"x_grouped{g}{c}")
-                if share:
-                    interleave(nc, "vector", grouped, x_raw[g, c], 0, share, 4)
-                interleave(nc, "scalar", grouped, x_raw[g, c], share, width, 4)
-                quantize(nc, x_codes[:, cols], x_scales[4 * g :, cols], grouped[:].rearrange("p c j -> p (c j)"))
-            picked = sb([P, S], U32, f"picked_codes{g}")
-            nc.vector.tensor_copy(out=picked[:], in_=x_codes[:].indirect(offs_sb[:]))
-            picked_codes.append(picked)
-        picked_scales = sb([P, S], U8, "picked_scales")
-        nc.vector.tensor_copy(out=picked_scales[:], in_=x_scales[:].indirect(offs_sb[:]))
+        picked_pairs = [sb([P, 2, S], U32, f"picked_pairs{g}") for g in range(PASSES)]
+        picked_codes, picked_scales = [], []
 
-        m_chunk = W_CHUNK // PACK
-        w1_grouped = []
-        for g in range(PASSES):
-            grouped = sb([P, PACK, P, PACK], BF16, f"w1_grouped{g}")
-            for c in range(H // W_CHUNK):
-                src = w1_raw[g, c][:].rearrange("p j (m t) -> p m j t", t=PACK)
-                dst = grouped[:, :, c * m_chunk : (c + 1) * m_chunk, :].rearrange("p t m j -> p m j t")
-                if g == PASSES - 1:
-                    cast(nc, "vector" if c == H // W_CHUNK - 1 else "scalar", dst[:, :, :, 0:2], src[:, :, :, 0:2])
-                    cast(nc, "scalar", dst[:, :, :, 2:4], src[:, :, :, 2:4])
-                else:
-                    cast(nc, "scalar", dst, src)
-            w1_grouped.append(grouped)
-        w1_codes, w1_scales = {}, {}
-        for g, t0, t1, tag in ((0, 0, 2, None), (1, 0, 1, None), (1, 1, 2, None), (1, 2, 4, None), (0, 2, 4, "w1_grouped1")):
+        def gather_pair(n):
+            pairs = sb([P, T, 2], BF16, f"x_pairs{n}")
+            interleave(nc, "vector", pairs, x_raw[n], 0, X_SHARES[n], 4)
+            interleave(nc, "scalar", pairs, x_raw[n], X_SHARES[n], T, 4)
+            window = pairs[:].rearrange("p c e -> p (c e)").bitcast(U32)
+            nc.vector.tensor_copy(out=picked_pairs[n // 2][:, n % 2, :], in_=window.indirect(offs_sb[:]))
+
+        def quantize_picked(g):
+            grouped = sb([P, S * PACK], BF16, f"x_grouped{g}", "x_raw10" if g == 0 else None)
+            if g == 0:
+                nc.scalar.copy(grouped[:].bitcast(U32).rearrange("p (c u) -> p c u", u=2), picked_pairs[g][:].rearrange("p u c -> p c u"))
+            else:
+                nc.vector.tensor_copy(
+                    out=grouped[:].bitcast(I32).rearrange("p (c u) -> p c u", u=2),
+                    in_=picked_pairs[g][:].bitcast(I32).rearrange("p u c -> p c u"),
+                )
+            codes = sb([P, S], U32, f"picked_codes{g}", "w1_grouped00" if g == 1 else None)
+            scales = sb([P, S], U8, f"picked_scales{g}")
+            quantize(nc, codes[:], scales[:], grouped[:])
+            picked_codes.append(codes)
+            picked_scales.append(scales)
+
+        w1_grouped, w1_codes, w1_scales = {}, {}, {}
+
+        def round_w1(g, u):
+            grouped = sb([P, 2, P, PACK], BF16, f"w1_grouped{g}{u}")
+            src = w1_raw[g][:].rearrange("p j (m t) -> p m j t", t=PACK)[:, :, :, 2 * u : 2 * u + 2]
+            dst = grouped[:].rearrange("p t m j -> p m j t")
+            if g == PASSES - 1:
+                share = (W_FIRST_SHARE, W_SECOND_SHARE)[u]
+                cast(nc, "vector", dst[:, :share], src[:, :share])
+                cast(nc, "scalar", dst[:, share:], src[:, share:])
+            else:
+                cast(nc, "scalar", dst, src)
+            w1_grouped[g, u] = grouped
+
+        def quantize_w1(g, t0, t1, tag=None):
             codes = sb([P, t1 - t0, P], U32, f"w1_codes{g}{t0}", tag)
             scales = sb([P, t1 - t0, P], U8, f"w1_scales{g}{t0}")
             quantize(
                 nc,
                 codes[:].rearrange("p t m -> p (t m)"),
                 scales[:].rearrange("p t m -> p (t m)"),
-                w1_grouped[g][:, t0:t1, :, :].rearrange("p t m j -> p (t m j)"),
+                w1_grouped[g, t0 // 2][:, t0 % 2 : t0 % 2 + t1 - t0, :, :].rearrange("p t m j -> p (t m j)"),
             )
             for t in range(t0, t1):
                 w1_codes[g, t] = codes[:, t - t0, :]
                 w1_scales[g, t] = scales[:, t - t0, :]
+
+        gather_pair(0)
+        gather_pair(1)
+        gather_pair(2)
+        quantize_picked(0)
+        gather_pair(3)
+        round_w1(0, 0)
+        round_w1(0, 1)
+        quantize_w1(0, 0, 2)
+        quantize_picked(1)
+        round_w1(1, 0)
+        round_w1(1, 1)
+        quantize_w1(1, 0, 1)
+        quantize_w1(1, 1, 2)
+        quantize_w1(0, 2, 4, "w1_grouped10")
+        quantize_w1(1, 2, 4)
 
         h = []
         for t in range(PACK):
@@ -150,7 +170,7 @@ def tile_picked_sagecat_max_e_kernel(tc, xT, w1, w2, w3, offs, cen, pos1, pos2, 
             banks = [psum.tile([P, cols.stop - cols.start], F32, name=f"h_bank{t}{n}", tag=f"h_bank{t}{n}") for n, cols in enumerate(pieces)]
             for g in range(PASSES):
                 for bank, cols in zip(banks, pieces):
-                    mx_pass(nc, bank[:], w1_codes[g, t], w1_scales[g, t], picked_codes[g][:, cols], picked_scales[4 * g :, cols], g == 0, g == PASSES - 1)
+                    mx_pass(nc, bank[:], w1_codes[g, t], w1_scales[g, t], picked_codes[g][:, cols], picked_scales[g][:, cols], g == 0, g == PASSES - 1)
             for n, (bank, cols) in enumerate(zip(banks, pieces)):
                 if n == 1:
                     nc.vector.tensor_scalar_max(h_t[:, cols], bank[:], 0.0)
@@ -165,7 +185,7 @@ def tile_picked_sagecat_max_e_kernel(tc, xT, w1, w2, w3, offs, cen, pos1, pos2, 
             nc.vector.tensor_copy(out=second[:, t, :], in_=h[t][:].indirect(pos2_sb[:]))
 
         out_w = []
-        for raw, name, tag in ((w3_raw, "w3", "picked_codes1"), (w2_raw, "w2", "w1_codes12")):
+        for raw, name, tag in ((w3_raw, "w3", "w1_grouped00"), (w2_raw, "w2", "w1_codes12")):
             grouped = sb([P, N, PACK], BF16, name + "_grouped", tag)
             interleave(nc, "scalar", grouped, raw, 0, N, 4)
             codes = sb([P, N], U32, name + "_codes")
@@ -187,7 +207,7 @@ def tile_picked_sagecat_max_e_kernel(tc, xT, w1, w2, w3, offs, cen, pos1, pos2, 
         for half in range(2):
             cols = slice(half * V_HALF, (half + 1) * V_HALF)
             offsets = cen_sb[:, half * (V_HALF // 16) : (half + 1) * (V_HALF // 16)]
-            own = sb([P, PACK, V_HALF], BF16, f"own{half}", "first" if half == 0 else "z_grouped")
+            own = sb([P, PACK, V_HALF], F32, f"own{half}", "first" if half == 0 else "z_grouped")
             for t in range(PACK):
                 nc.vector.tensor_copy(out=own[:, t, :], in_=h[t][:].indirect(offsets))
             if half == 0:

@@ -20,7 +20,7 @@ P = 128
 PACK = 4
 K_PASS = P * PACK
 PASSES = K // K_PASS
-X_SHARES = (640, 640, 640, 512)
+X_SHARES = (640, 640, 640, 640)
 W_FIRST_SHARE = 80
 W_SECOND_SHARE = 64
 V_HALF = V // 2
@@ -105,7 +105,9 @@ def tile_picked_sagecat_max_e_kernel(tc, xT, w1, w2, w3, offs, cen, pos1, pos2, 
             window = pairs[:].rearrange("p c e -> p (c e)").bitcast(U32)
             nc.vector.tensor_copy(out=picked_pairs[n // 2][:, n % 2, :], in_=window.indirect(offs_sb[:]))
 
-        def quantize_picked(g):
+        x_grouped = []
+
+        def weave_picked(g):
             grouped = sb([P, S * PACK], BF16, f"x_grouped{g}", "x_raw10" if g == 0 else None)
             if g == 0:
                 nc.scalar.copy(grouped[:].bitcast(U32).rearrange("p (c u) -> p c u", u=2), picked_pairs[g][:].rearrange("p u c -> p c u"))
@@ -114,7 +116,11 @@ def tile_picked_sagecat_max_e_kernel(tc, xT, w1, w2, w3, offs, cen, pos1, pos2, 
                     out=grouped[:].bitcast(I32).rearrange("p (c u) -> p c u", u=2),
                     in_=picked_pairs[g][:].bitcast(I32).rearrange("p u c -> p c u"),
                 )
-            codes = sb([P, S], U32, f"picked_codes{g}", "w1_grouped00" if g == 1 else None)
+            x_grouped.append(grouped)
+
+        def quantize_picked(g):
+            grouped = x_grouped[g]
+            codes = sb([P, S], U32, f"picked_codes{g}", ("x_pairs3", "w1_grouped00")[g])
             scales = sb([P, S], U8, f"picked_scales{g}")
             quantize(nc, codes[:], scales[:], grouped[:])
             picked_codes.append(codes)
@@ -150,8 +156,10 @@ def tile_picked_sagecat_max_e_kernel(tc, xT, w1, w2, w3, offs, cen, pos1, pos2, 
         gather_pair(0)
         gather_pair(1)
         gather_pair(2)
-        quantize_picked(0)
+        weave_picked(0)
         gather_pair(3)
+        quantize_picked(0)
+        weave_picked(1)
         round_w1(0, 0)
         round_w1(0, 1)
         quantize_w1(0, 0, 2)
@@ -178,8 +186,8 @@ def tile_picked_sagecat_max_e_kernel(tc, xT, w1, w2, w3, offs, cen, pos1, pos2, 
                     nc.scalar.activation(h_t[:, cols], bank[:], RELU)
             h.append(h_t)
 
-        first = sb([P, PACK, V], BF16, "first")
-        second = sb([P, PACK, V], BF16, "second")
+        first = sb([P, PACK, V], F32, "first")
+        second = sb([P, PACK, V], F32, "second")
         for t in range(PACK):
             nc.vector.tensor_copy(out=first[:, t, :], in_=h[t][:].indirect(pos1_sb[:]))
             nc.vector.tensor_copy(out=second[:, t, :], in_=h[t][:].indirect(pos2_sb[:]))
@@ -194,24 +202,31 @@ def tile_picked_sagecat_max_e_kernel(tc, xT, w1, w2, w3, offs, cen, pos1, pos2, 
             out_w.append((codes, scales))
         (w3_codes, w3_scales), (w2_codes, w2_scales) = out_w
 
-        z = sb([P, PACK, V], BF16, "z")
+        first_grouped = sb([P, V, PACK], BF16, "first_grouped")
+        second_grouped = sb([P, V, PACK], BF16, "second_grouped")
         z_grouped = sb([P, V, PACK], BF16, "z_grouped")
-        for lo in range(0, V, V_HALF):
-            hi = lo + V_HALF
-            nc.vector.tensor_tensor(z[:, :, lo:hi], first[:, :, lo:hi], second[:, :, lo:hi], MAX)
-            interleave(nc, "scalar", z_grouped, z, lo, hi, 4)
+        for planes, grouped in ((first, first_grouped), (second, second_grouped)):
+            for lo in range(0, V, V_HALF):
+                interleave(nc, "scalar", grouped, planes, lo, lo + V_HALF, 4)
         z_codes = sb([P, V], U32, "z_codes")
         z_scales = sb([P, V], U8, "z_scales")
 
         out_rows = out.rearrange("(a p) v -> p a v", p=P)
+        own_mx = []
         for half in range(2):
-            cols = slice(half * V_HALF, (half + 1) * V_HALF)
             offsets = cen_sb[:, half * (V_HALF // 16) : (half + 1) * (V_HALF // 16)]
-            own = sb([P, PACK, V_HALF], F32, f"own{half}", "first" if half == 0 else "z_grouped")
+            if half == 0:
+                own = first[:, :, 0:V_HALF]
+            else:
+                own = sb([P, PACK, V_HALF], F32, "own1", "second_grouped")[:]
             for t in range(PACK):
                 nc.vector.tensor_copy(out=own[:, t, :], in_=h[t][:].indirect(offsets))
+                if half == 1 and t == 0:
+                    quantize(nc, z_codes[:], z_scales[:], z_grouped[:].rearrange("p c j -> p (c j)"))
             if half == 0:
-                quantize(nc, z_codes[:], z_scales[:], z_grouped[:].rearrange("p c j -> p (c j)"))
+                for lo in range(0, V, V_HALF):
+                    hi = lo + V_HALF
+                    nc.vector.tensor_tensor(z_grouped[:, lo:hi, :], first_grouped[:, lo:hi, :], second_grouped[:, lo:hi, :], MAX)
             own_grouped = sb([P, V_HALF, PACK], BF16, f"own_grouped{half}")
             pieces = [(0, V_HALF)] if half == 0 else [(0, V_HALF // 2), (V_HALF // 2, V_HALF)]
             for lo, hi in pieces:
@@ -220,7 +235,10 @@ def tile_picked_sagecat_max_e_kernel(tc, xT, w1, w2, w3, offs, cen, pos1, pos2, 
             own_scales = sb([P, V_HALF], U8, f"own_scales{half}")
             for lo, hi in pieces:
                 quantize(nc, own_codes[:, lo:hi], own_scales[:, lo:hi], own_grouped[:, lo:hi, :].rearrange("p c j -> p (c j)"))
+            own_mx.append((own_codes, own_scales))
 
+        for half, (own_codes, own_scales) in enumerate(own_mx):
+            cols = slice(half * V_HALF, (half + 1) * V_HALF)
             bank_tags = ("h_bank00", "h_bank01") if half == 0 else ("out_bank0", "out_bank1")
             banks = [psum.tile([P, V_HALF], F32, name=f"out_bank{half}{a}", tag=bank_tags[a]) for a in range(2)]
             for a in range(2):

from contextlib import ExitStack

import concourse.mybir as mybir

K, T, S, V, H, N = 1024, 1024, 512, 256, 512, 256
FLOPS = 2 * K * H * S + 2 * 2 * H * N * V

F32 = mybir.dt.float32
BF16 = mybir.dt.bfloat16
U32 = mybir.dt.uint32
I32 = mybir.dt.int32
U16 = mybir.dt.uint16
U8 = mybir.dt.uint8
FP8X4 = mybir.dt.float8_e4m3fn_x4
COPY = mybir.ActivationFunctionType.Copy
RELU = mybir.ActivationFunctionType.Relu
MAX = mybir.AluOpType.max

P = 128
PACK = 4
K_PASS = P * PACK
PASSES = K // K_PASS
X_SHARES = (640, 640, 640, 640)
W_FIRST_SHARE = 80
W_SECOND_SHARE = 64
V_HALF = V // 2


def cast(nc, engine, out, in_):
    if engine == "vector":
        nc.vector.tensor_copy(out=out, in_=in_)
    else:
        nc.scalar.activation(out, in_, COPY)


def interleave(nc, engine, grouped, planes, lo, hi, run):
    cast(
        nc,
        engine,
        grouped[:, lo:hi, :].rearrange("p (c i) j -> p c j i", i=run),
        planes[:, :, lo:hi].rearrange("p j (c i) -> p c j i", i=run),
    )


def quantize(nc, codes, scales, grouped):
    nc.vector.quantize_mx(out=codes.bitcast(FP8X4), scales=scales, in_=grouped)


def mx_pass(nc, out, lhs_codes, lhs_scales, rhs_codes, rhs_scales, start, stop):
    nc.tensor.matmul_mx(
        out=out,
        lhsT=lhs_codes.bitcast(FP8X4),
        lhsT_scale=lhs_scales,
        rhs=rhs_codes.bitcast(FP8X4),
        rhs_scale=rhs_scales,
        start=start,
        stop=stop,
    )


def tile_picked_sagecat_max_e_kernel(tc, xT, w1, w2, w3, offs, cen, pos1, pos2, out):
    nc = tc.nc
    with ExitStack() as ctx:
        lists = ctx.enter_context(tc.tile_pool(name="lists", bufs=1))
        pool = ctx.enter_context(tc.tile_pool(name="sbuf", bufs=1))
        psum = ctx.enter_context(tc.psum_pool(name="psum", bufs=1))

        def sb(shape, dtype, name, tag=None):
            return pool.tile(shape, dtype, name=name, tag=tag or name, align_bytes=64)

        def load_list(src, name):
            tile = lists.tile(list(src.shape), U16, name=name, tag=name)
            nc.sync.dma_start(tile[:], src)
            return tile

        x_raw = []
        for g in range(PASSES):
            rows = xT[g * K_PASS : (g + 1) * K_PASS, :].rearrange("(p j) c -> p j c", j=PACK)
            for u in range(2):
                raw = sb([P, 2, T], F32, f"x_raw{g}{u}")
                nc.sync.dma_start(out=raw[:], in_=rows[:, 2 * u : 2 * u + 2, :])
                x_raw.append(raw)
                if (g, u) == (0, 0):
                    offs_sb = load_list(offs, "offs_sb")
        w1_raw = []
        for g in range(PASSES):
            raw = sb([P, PACK, H], F32, f"w1_raw{g}")
            nc.sync.dma_start(out=raw[:], in_=w1[g * K_PASS : (g + 1) * K_PASS, :].rearrange("(p j) c -> p j c", j=PACK))
            w1_raw.append(raw)
        pos1_sb = load_list(pos1, "pos1_sb")
        pos2_sb = load_list(pos2, "pos2_sb")
        cen_sb = load_list(cen, "cen_sb")
        w3_raw = sb([P, PACK, N], F32, "w3_raw")
        nc.sync.dma_start(out=w3_raw[:], in_=w3.rearrange("(p j) c -> p j c", j=PACK))
        w2_raw = sb([P, PACK, N], F32, "w2_raw")
        nc.sync.dma_start(out=w2_raw[:], in_=w2.rearrange("(p j) c -> p j c", j=PACK))

        picked_pairs = [sb([P, 2, S], U32, f"picked_pairs{g}") for g in range(PASSES)]
        picked_codes, picked_scales = [], []

        def gather_pair(n):
            pairs = sb([P, T, 2], BF16, f"x_pairs{n}")
            interleave(nc, "vector", pairs, x_raw[n], 0, X_SHARES[n], 4)
            interleave(nc, "scalar", pairs, x_raw[n], X_SHARES[n], T, 4)
            window = pairs[:].rearrange("p c e -> p (c e)").bitcast(U32)
            nc.vector.tensor_copy(out=picked_pairs[n // 2][:, n % 2, :], in_=window.indirect(offs_sb[:]))

        x_grouped = []

        def weave_picked(g):
            grouped = sb([P, S * PACK], BF16, f"x_grouped{g}", "x_raw10" if g == 0 else None)
            if g == 0:
                nc.scalar.copy(grouped[:].bitcast(U32).rearrange("p (c u) -> p c u", u=2), picked_pairs[g][:].rearrange("p u c -> p c u"))
            else:
                nc.vector.tensor_copy(
                    out=grouped[:].bitcast(I32).rearrange("p (c u) -> p c u", u=2),
                    in_=picked_pairs[g][:].bitcast(I32).rearrange("p u c -> p c u"),
                )
            x_grouped.append(grouped)

        def quantize_picked(g):
            grouped = x_grouped[g]
            codes = sb([P, S], U32, f"picked_codes{g}", ("x_pairs3", "w1_grouped00")[g])
            scales = sb([P, S], U8, f"picked_scales{g}")
            quantize(nc, codes[:], scales[:], grouped[:])
            picked_codes.append(codes)
            picked_scales.append(scales)

        w1_grouped, w1_codes, w1_scales = {}, {}, {}

        def round_w1(g, u):
            grouped = sb([P, 2, P, PACK], BF16, f"w1_grouped{g}{u}")
            src = w1_raw[g][:].rearrange("p j (m t) -> p m j t", t=PACK)[:, :, :, 2 * u : 2 * u + 2]
            dst = grouped[:].rearrange("p t m j -> p m j t")
            if g == PASSES - 1:
                share = (W_FIRST_SHARE, W_SECOND_SHARE)[u]
                cast(nc, "vector", dst[:, :share], src[:, :share])
                cast(nc, "scalar", dst[:, share:], src[:, share:])
            else:
                cast(nc, "scalar", dst, src)
            w1_grouped[g, u] = grouped

        def quantize_w1(g, t0, t1, tag=None):
            codes = sb([P, t1 - t0, P], U32, f"w1_codes{g}{t0}", tag)
            scales = sb([P, t1 - t0, P], U8, f"w1_scales{g}{t0}")
            quantize(
                nc,
                codes[:].rearrange("p t m -> p (t m)"),
                scales[:].rearrange("p t m -> p (t m)"),
                w1_grouped[g, t0 // 2][:, t0 % 2 : t0 % 2 + t1 - t0, :, :].rearrange("p t m j -> p (t m j)"),
            )
            for t in range(t0, t1):
                w1_codes[g, t] = codes[:, t - t0, :]
                w1_scales[g, t] = scales[:, t - t0, :]

        gather_pair(0)
        gather_pair(1)
        gather_pair(2)
        weave_picked(0)
        gather_pair(3)
        quantize_picked(0)
        weave_picked(1)
        round_w1(0, 0)
        round_w1(0, 1)
        quantize_w1(0, 0, 2)
        quantize_picked(1)
        round_w1(1, 0)
        round_w1(1, 1)
        quantize_w1(1, 0, 1)
        quantize_w1(1, 1, 2)
        quantize_w1(0, 2, 4, "w1_grouped10")
        quantize_w1(1, 2, 4)

        h = []
        for t in range(PACK):
            h_t = sb([P, S], F32, f"h{t}")
            pieces = [slice(0, S // 2), slice(S // 2, S)] if t == 0 else [slice(0, S)]
            banks = [psum.tile([P, cols.stop - cols.start], F32, name=f"h_bank{t}{n}", tag=f"h_bank{t}{n}") for n, cols in enumerate(pieces)]
            for g in range(PASSES):
                for bank, cols in zip(banks, pieces):
                    mx_pass(nc, bank[:], w1_codes[g, t], w1_scales[g, t], picked_codes[g][:, cols], picked_scales[g][:, cols], g == 0, g == PASSES - 1)
            for n, (bank, cols) in enumerate(zip(banks, pieces)):
                if n == 1:
                    nc.vector.tensor_scalar_max(h_t[:, cols], bank[:], 0.0)
                else:
                    nc.scalar.activation(h_t[:, cols], bank[:], RELU)
            h.append(h_t)

        first = sb([P, PACK, V], F32, "first")
        second = sb([P, PACK, V], F32, "second")
        for t in range(PACK):
            nc.vector.tensor_copy(out=first[:, t, :], in_=h[t][:].indirect(pos1_sb[:]))
            nc.vector.tensor_copy(out=second[:, t, :], in_=h[t][:].indirect(pos2_sb[:]))

        out_w = []
        for raw, name, tag in ((w3_raw, "w3", "w1_grouped00"), (w2_raw, "w2", "w1_codes12")):
            grouped = sb([P, N, PACK], BF16, name + "_grouped", tag)
            interleave(nc, "scalar", grouped, raw, 0, N, 4)
            codes = sb([P, N], U32, name + "_codes")
            scales = sb([P, N], U8, name + "_scales")
            quantize(nc, codes[:], scales[:], grouped[:].rearrange("p c j -> p (c j)"))
            out_w.append((codes, scales))
        (w3_codes, w3_scales), (w2_codes, w2_scales) = out_w

        first_grouped = sb([P, V, PACK], BF16, "first_grouped")
        second_grouped = sb([P, V, PACK], BF16, "second_grouped")
        z_grouped = sb([P, V, PACK], BF16, "z_grouped")
        for planes, grouped in ((first, first_grouped), (second, second_grouped)):
            for lo in range(0, V, V_HALF):
                interleave(nc, "scalar", grouped, planes, lo, lo + V_HALF, 4)
        z_codes = sb([P, V], U32, "z_codes")
        z_scales = sb([P, V], U8, "z_scales")

        out_rows = out.rearrange("(a p) v -> p a v", p=P)
        own_mx = []
        for half in range(2):
            offsets = cen_sb[:, half * (V_HALF // 16) : (half + 1) * (V_HALF // 16)]
            if half == 0:
                own = first[:, :, 0:V_HALF]
            else:
                own = sb([P, PACK, V_HALF], F32, "own1", "second_grouped")[:]
            for t in range(PACK):
                nc.vector.tensor_copy(out=own[:, t, :], in_=h[t][:].indirect(offsets))
                if half == 1 and t == 0:
                    quantize(nc, z_codes[:], z_scales[:], z_grouped[:].rearrange("p c j -> p (c j)"))
            if half == 0:
                for lo in range(0, V, V_HALF):
                    hi = lo + V_HALF
                    nc.vector.tensor_tensor(z_grouped[:, lo:hi, :], first_grouped[:, lo:hi, :], second_grouped[:, lo:hi, :], MAX)
            own_grouped = sb([P, V_HALF, PACK], BF16, f"own_grouped{half}")
            pieces = [(0, V_HALF)] if half == 0 else [(0, V_HALF // 2), (V_HALF // 2, V_HALF)]
            for lo, hi in pieces:
                interleave(nc, "scalar" if half == 0 else "vector", own_grouped, own, lo, hi, 4)
            own_codes = sb([P, V_HALF], U32, f"own_codes{half}")
            own_scales = sb([P, V_HALF], U8, f"own_scales{half}")
            for lo, hi in pieces:
                quantize(nc, own_codes[:, lo:hi], own_scales[:, lo:hi], own_grouped[:, lo:hi, :].rearrange("p c j -> p (c j)"))
            own_mx.append((own_codes, own_scales))

        for half, (own_codes, own_scales) in enumerate(own_mx):
            cols = slice(half * V_HALF, (half + 1) * V_HALF)
            bank_tags = ("h_bank00", "h_bank01") if half == 0 else ("out_bank0", "out_bank1")
            banks = [psum.tile([P, V_HALF], F32, name=f"out_bank{half}{a}", tag=bank_tags[a]) for a in range(2)]
            for a in range(2):
                rows = slice(a * P, (a + 1) * P)
                mx_pass(nc, banks[a][:], w3_codes[:, rows], w3_scales[:, rows], z_codes[:, cols], z_scales[:, cols], True, False)
            for a in range(2):
                rows = slice(a * P, (a + 1) * P)
                mx_pass(nc, banks[a][:], w2_codes[:, rows], w2_scales[:, rows], own_codes[:], own_scales[:], False, True)
            if half == 0:
                result = sb([P, 2, V_HALF], F32, "result0")
                for a in range(2):
                    nc.scalar.copy(result[:, a, :], banks[a][:])
                nc.sync.dma_start(out=out_rows[:, :, cols], in_=result[:])
            else:
                result_a = sb([P, V_HALF], F32, "result10")
                nc.vector.tensor_copy(out=result_a[:], in_=banks[0][:])
                nc.sync.dma_start(out=out_rows[:, 0, cols], in_=result_a[:])
                result_b = sb([P, V_HALF], F32, "result11")
                nc.scalar.copy(result_b[:], banks[1][:])
                nc.scalar.dma_start(out=out_rows[:, 1, cols], in_=result_b[:])
